import numpy as np
import ml_dtypes

BF16 = ml_dtypes.bfloat16


def bf(x):
    return np.asarray(x, np.float32).astype(BF16)


def f32(x):
    return np.asarray(x, np.float32)


def f64(x):
    return np.asarray(x).astype(np.float64)


def striped(idx):
    return np.tile(idx.reshape(-1, 16).T, (8, 1))


S, K, M, N, D, V = 512, 128, 256, 768, 8, 96


def setup_inputs():
    return {"table": bf(np.random.standard_normal((K, S))), "w": bf(np.random.standard_normal((K, M)) / np.sqrt(K)), "b": f32(0.5 * np.random.standard_normal((M, 1))), "offs": striped(np.random.permutation(np.tile(np.arange(S), 2))[:N])}


def reference(table, w, b, offs):
    idx = offs[:16].T.reshape(-1)
    x = f64(table)[:, idx]
    y = f64(w).T @ x
    z = np.maximum(y + f64(b), 0.0)
    return z.reshape(M, V, D).max(axis=2)

@@ -1,0 +1,52 @@
+import concourse.mybir as mybir
+
+BF16, F32, U16 = mybir.dt.bfloat16, mybir.dt.float32, mybir.dt.uint16
+ADD, MAX = mybir.AluOpType.add, mybir.AluOpType.max
+
+P = 128
+S = 512
+M = 256
+N = 768
+D = 8
+PIECE = 256
+LANES = 16
+
+FLOPS = 2 * P * M * N
+
+
+def tile_gather_matmul_kernel(tc, table, w, b, offs, out):
+    nc = tc.nc
+    with (
+        tc.tile_pool(name="held", bufs=1) as held,
+        tc.psum_pool(name="banks", bufs=1) as banks,
+    ):
+        offsets = held.tile([P, N // LANES], U16, name="offsets")
+        nc.sync.dma_start(offsets[:], offs)
+        nodes = held.tile([P, S], BF16, name="nodes")
+        nc.scalar.dma_start(nodes[:], table)
+        weights = held.tile([P, M], BF16, name="weights")
+        nc.sync.dma_start(weights[:], w)
+        bias = held.tile([P, M // P], F32, name="bias")
+        with nc.allow_non_contiguous_dma(reason="one float32 to a partition and block"):
+            nc.scalar.dma_start(bias[:], b.rearrange("(a p) o -> p (a o)", p=P))
+
+        for a in range(M // P):
+            largest = held.tile([P, N // D], F32, name=f"largest{a}")
+            for q in range(N // PIECE):
+                product = banks.tile([P, PIECE], F32, name=f"product{a}_{q}")
+                nc.tensor.matmul(
+                    product[:],
+                    weights[:, a * P : (a + 1) * P],
+                    nodes[:].indirect(offsets[:, q * PIECE // LANES : (q + 1) * PIECE // LANES]),
+                    start=True,
+                    stop=True,
+                )
+                nc.vector.tensor_reduce(
+                    out=largest[:, q * PIECE // D : (q + 1) * PIECE // D],
+                    in_=product[:].rearrange("p (v t) -> p v t", t=D),
+                    axis=mybir.AxisListType.X,
+                    op=MAX,
+                )
+            pooled = held.tile([P, N // D], F32, name=f"pooled{a}")
+            nc.vector.tensor_scalar(pooled[:], largest[:], bias[:, a : a + 1], 0.0, op0=ADD, op1=MAX)
+            nc.sync.dma_start(out[a * P : (a + 1) * P, :], pooled[:])

@@ -2,6 +2,7 @@ import concourse.mybir as mybir
 
 BF16, F32, U16 = mybir.dt.bfloat16, mybir.dt.float32, mybir.dt.uint16
 ADD, MAX = mybir.AluOpType.add, mybir.AluOpType.max
+RELU = mybir.ActivationFunctionType.Relu
 
 P = 128
 S = 512
@@ -30,6 +31,11 @@ def tile_gather_matmul_kernel(tc, table, w, b, offs, out):
         with nc.allow_non_contiguous_dma(reason="one float32 to a partition and block"):
             nc.scalar.dma_start(bias[:], b.rearrange("(a p) o -> p (a o)", p=P))
 
+        zeros = held.tile([P, 1], F32, name="zeros")
+        nc.vector.memset(zeros[:], 0.0)
+        unused = held.tile([P, 1], F32, name="unused")
+        nc.scalar.activation(unused[:], zeros[:], RELU)
+
         for a in range(M // P):
             largest = held.tile([P, N // D], F32, name=f"largest{a}")
             for q in range(N // PIECE):
@@ -48,5 +54,8 @@ def tile_gather_matmul_kernel(tc, table, w, b, offs, out):
                     op=MAX,
                 )
             pooled = held.tile([P, N // D], F32, name=f"pooled{a}")
-            nc.vector.tensor_scalar(pooled[:], largest[:], bias[:, a : a + 1], 0.0, op0=ADD, op1=MAX)
+            if a < M // P - 1:
+                nc.scalar.activation(pooled[:], largest[:], RELU, bias=bias[:, a : a + 1])
+            else:
+                nc.vector.tensor_scalar(pooled[:], largest[:], bias[:, a : a + 1], 0.0, op0=ADD, op1=MAX)
             nc.sync.dma_start(out[a * P : (a + 1) * P, :], pooled[:])

@@ -21,12 +21,12 @@ def tile_gather_matmul_kernel(tc, table, w, b, offs, out):
         tc.tile_pool(name="held", bufs=1) as held,
         tc.psum_pool(name="banks", bufs=1) as banks,
     ):
+        nodes = held.tile([P, S], BF16, name="nodes")
+        nc.sync.dma_start(nodes[:], table)
         offsets = held.tile([P, N // LANES], U16, name="offsets")
         nc.sync.dma_start(offsets[:], offs)
-        nodes = held.tile([P, S], BF16, name="nodes")
-        nc.scalar.dma_start(nodes[:], table)
         weights = held.tile([P, M], BF16, name="weights")
-        nc.sync.dma_start(weights[:], w)
+        nc.scalar.dma_start(weights[:], w)
         bias = held.tile([P, M // P], F32, name="bias")
         with nc.allow_non_contiguous_dma(reason="one float32 to a partition and block"):
             nc.scalar.dma_start(bias[:], b.rearrange("(a p) o -> p (a o)", p=P))

@@ -7,10 +7,14 @@ RELU = mybir.ActivationFunctionType.Relu
 P = 128
 S = 512
 M = 256
+A = M // P
 N = 768
 D = 8
+V = N // D
 PIECE = 256
+PIECES = N // PIECE
 LANES = 16
+LATE = 2
 
 FLOPS = 2 * P * M * N
 
@@ -27,35 +31,43 @@ def tile_gather_matmul_kernel(tc, table, w, b, offs, out):
         nc.sync.dma_start(offsets[:], offs)
         weights = held.tile([P, M], BF16, name="weights")
         nc.scalar.dma_start(weights[:], w)
-        bias = held.tile([P, M // P], F32, name="bias")
-        with nc.allow_non_contiguous_dma(reason="one float32 to a partition and block"):
-            nc.scalar.dma_start(bias[:], b.rearrange("(a p) o -> p (a o)", p=P))
+        bias = held.tile([P, A], F32, name="bias")
+        nc.scalar.dma_start(bias[:], b.rearrange("(p a) o -> p (a o)", a=A))
 
         zeros = held.tile([P, 1], F32, name="zeros")
         nc.vector.memset(zeros[:], 0.0)
         unused = held.tile([P, 1], F32, name="unused")
         nc.scalar.activation(unused[:], zeros[:], RELU)
 
-        for a in range(M // P):
-            largest = held.tile([P, N // D], F32, name=f"largest{a}")
-            for q in range(N // PIECE):
+        early_cols = A * V - LATE * PIECE // D
+        early_max = held.tile([P, early_cols], F32, name="early_max")
+        late_max = held.tile([P, A * V - early_cols], F32, name="late_max")
+        for a in range(A):
+            for q in range(PIECES):
                 product = banks.tile([P, PIECE], F32, name=f"product{a}_{q}")
                 nc.tensor.matmul(
                     product[:],
-                    weights[:, a * P : (a + 1) * P],
+                    weights[:, a::A],
                     nodes[:].indirect(offsets[:, q * PIECE // LANES : (q + 1) * PIECE // LANES]),
                     start=True,
                     stop=True,
                 )
+                first = (a * PIECES + q) * PIECE // D
+                if first < early_cols:
+                    largest = early_max[:, first : first + PIECE // D]
+                else:
+                    largest = late_max[:, first - early_cols : first - early_cols + PIECE // D]
                 nc.vector.tensor_reduce(
-                    out=largest[:, q * PIECE // D : (q + 1) * PIECE // D],
+                    out=largest,
                     in_=product[:].rearrange("p (v t) -> p v t", t=D),
                     axis=mybir.AxisListType.X,
                     op=MAX,
                 )
-            pooled = held.tile([P, N // D], F32, name=f"pooled{a}")
-            if a < M // P - 1:
-                nc.scalar.activation(pooled[:], largest[:], RELU, bias=bias[:, a : a + 1])
-            else:
-                nc.vector.tensor_scalar(pooled[:], largest[:], bias[:, a : a + 1], 0.0, op0=ADD, op1=MAX)
-            nc.sync.dma_start(out[a * P : (a + 1) * P, :], pooled[:])
+        early = held.tile([P, early_cols], F32, name="early")
+        late = held.tile([P, A * V - early_cols], F32, name="late")
+        nc.scalar.activation(early[:, :V], early_max[:, :V], RELU, bias=bias[:, 0:1])
+        nc.scalar.activation(early[:, V:], early_max[:, V:], RELU, bias=bias[:, 1:2])
+        rows = out.rearrange("(p a) v -> p (a v)", a=A)
+        nc.sync.dma_start(rows[:, :early_cols], early[:])
+        nc.vector.tensor_scalar(late[:], late_max[:], bias[:, 1:2], 0.0, op0=ADD, op1=MAX)
+        nc.sync.dma_start(rows[:, early_cols:], late[:])

@@ -1,7 +1,7 @@
 import concourse.mybir as mybir
 
 BF16, F32, U16 = mybir.dt.bfloat16, mybir.dt.float32, mybir.dt.uint16
-ADD, MAX = mybir.AluOpType.add, mybir.AluOpType.max
+MAX = mybir.AluOpType.max
 RELU = mybir.ActivationFunctionType.Relu
 
 P = 128
@@ -14,7 +14,7 @@ V = N // D
 PIECE = 256
 PIECES = N // PIECE
 LANES = 16
-LATE = 2
+EARLY = 4
 
 FLOPS = 2 * P * M * N
 
@@ -39,35 +39,33 @@ def tile_gather_matmul_kernel(tc, table, w, b, offs, out):
         unused = held.tile([P, 1], F32, name="unused")
         nc.scalar.activation(unused[:], zeros[:], RELU)
 
-        early_cols = A * V - LATE * PIECE // D
-        early_max = held.tile([P, early_cols], F32, name="early_max")
-        late_max = held.tile([P, A * V - early_cols], F32, name="late_max")
-        for a in range(A):
-            for q in range(PIECES):
-                product = banks.tile([P, PIECE], F32, name=f"product{a}_{q}")
-                nc.tensor.matmul(
-                    product[:],
-                    weights[:, a::A],
-                    nodes[:].indirect(offsets[:, q * PIECE // LANES : (q + 1) * PIECE // LANES]),
-                    start=True,
-                    stop=True,
-                )
-                first = (a * PIECES + q) * PIECE // D
-                if first < early_cols:
-                    largest = early_max[:, first : first + PIECE // D]
-                else:
-                    largest = late_max[:, first - early_cols : first - early_cols + PIECE // D]
-                nc.vector.tensor_reduce(
-                    out=largest,
-                    in_=product[:].rearrange("p (v t) -> p v t", t=D),
-                    axis=mybir.AxisListType.X,
-                    op=MAX,
-                )
+        early_cols = EARLY * PIECE // D
         early = held.tile([P, early_cols], F32, name="early")
         late = held.tile([P, A * V - early_cols], F32, name="late")
-        nc.scalar.activation(early[:, :V], early_max[:, :V], RELU, bias=bias[:, 0:1])
-        nc.scalar.activation(early[:, V:], early_max[:, V:], RELU, bias=bias[:, 1:2])
         rows = out.rearrange("(p a) v -> p (a v)", a=A)
-        nc.sync.dma_start(rows[:, :early_cols], early[:])
-        nc.vector.tensor_scalar(late[:], late_max[:], bias[:, 1:2], 0.0, op0=ADD, op1=MAX)
+        for piece in range(A * PIECES):
+            a, q = divmod(piece, PIECES)
+            product = banks.tile([P, PIECE], F32, name=f"product{piece}")
+            nc.tensor.matmul(
+                product[:],
+                weights[:, a::A],
+                nodes[:].indirect(offsets[:, q * PIECE // LANES : (q + 1) * PIECE // LANES]),
+                start=True,
+                stop=True,
+            )
+            largest = held.tile([P, PIECE // D], F32, name=f"largest{piece}")
+            nc.vector.tensor_reduce(
+                out=largest[:],
+                in_=product[:].rearrange("p (v t) -> p v t", t=D),
+                axis=mybir.AxisListType.X,
+                op=MAX,
+            )
+            first = piece * PIECE // D
+            if piece < EARLY:
+                pooled = early[:, first : first + PIECE // D]
+            else:
+                pooled = late[:, first - early_cols : first - early_cols + PIECE // D]
+            nc.scalar.activation(pooled, largest[:], RELU, bias=bias[:, a : a + 1])
+            if piece == EARLY - 1:
+                nc.sync.dma_start(rows[:, :early_cols], early[:])
         nc.sync.dma_start(rows[:, early_cols:], late[:])

@@ -11,10 +11,11 @@ A = M // P
 N = 768
 D = 8
 V = N // D
-PIECE = 256
+PIECE = 128
 PIECES = N // PIECE
+BANKS = 8
 LANES = 16
-EARLY = 4
+EARLY = 8
 
 FLOPS = 2 * P * M * N
 
@@ -23,7 +24,7 @@ def tile_gather_matmul_kernel(tc, table, w, b, offs, out):
     nc = tc.nc
     with (
         tc.tile_pool(name="held", bufs=1) as held,
-        tc.psum_pool(name="banks", bufs=1) as banks,
+        tc.psum_pool(name="banks", bufs=BANKS) as banks,
     ):
         nodes = held.tile([P, S], BF16, name="nodes")
         nc.sync.dma_start(nodes[:], table)
@@ -45,7 +46,7 @@ def tile_gather_matmul_kernel(tc, table, w, b, offs, out):
         rows = out.rearrange("(p a) v -> p (a v)", a=A)
         for piece in range(A * PIECES):
             a, q = divmod(piece, PIECES)
-            product = banks.tile([P, PIECE], F32, name=f"product{piece}")
+            product = banks.tile([P, PIECE], F32, name="product")
             nc.tensor.matmul(
                 product[:],
                 weights[:, a::A],

import concourse.mybir as mybir

BF16, F32, U16 = mybir.dt.bfloat16, mybir.dt.float32, mybir.dt.uint16
MAX = mybir.AluOpType.max
RELU = mybir.ActivationFunctionType.Relu

P = 128
S = 512
M = 256
A = M // P
N = 768
D = 8
V = N // D
PIECE = 128
PIECES = N // PIECE
BANKS = 8
LANES = 16
EARLY = 8

FLOPS = 2 * P * M * N


def tile_gather_matmul_kernel(tc, table, w, b, offs, out):
    nc = tc.nc
    with (
        tc.tile_pool(name="held", bufs=1) as held,
        tc.psum_pool(name="banks", bufs=BANKS) as banks,
    ):
        nodes = held.tile([P, S], BF16, name="nodes")
        nc.sync.dma_start(nodes[:], table)
        offsets = held.tile([P, N // LANES], U16, name="offsets")
        nc.sync.dma_start(offsets[:], offs)
        weights = held.tile([P, M], BF16, name="weights")
        nc.scalar.dma_start(weights[:], w)
        bias = held.tile([P, A], F32, name="bias")
        nc.scalar.dma_start(bias[:], b.rearrange("(p a) o -> p (a o)", a=A))

        zeros = held.tile([P, 1], F32, name="zeros")
        nc.vector.memset(zeros[:], 0.0)
        unused = held.tile([P, 1], F32, name="unused")
        nc.scalar.activation(unused[:], zeros[:], RELU)

        early_cols = EARLY * PIECE // D
        early = held.tile([P, early_cols], F32, name="early")
        late = held.tile([P, A * V - early_cols], F32, name="late")
        rows = out.rearrange("(p a) v -> p (a v)", a=A)
        for piece in range(A * PIECES):
            a, q = divmod(piece, PIECES)
            product = banks.tile([P, PIECE], F32, name="product")
            nc.tensor.matmul(
                product[:],
                weights[:, a::A],
                nodes[:].indirect(offsets[:, q * PIECE // LANES : (q + 1) * PIECE // LANES]),
                start=True,
                stop=True,
            )
            largest = held.tile([P, PIECE // D], F32, name=f"largest{piece}")
            nc.vector.tensor_reduce(
                out=largest[:],
                in_=product[:].rearrange("p (v t) -> p v t", t=D),
                axis=mybir.AxisListType.X,
                op=MAX,
            )
            first = piece * PIECE // D
            if piece < EARLY:
                pooled = early[:, first : first + PIECE // D]
            else:
                pooled = late[:, first - early_cols : first - early_cols + PIECE // D]
            nc.scalar.activation(pooled, largest[:], RELU, bias=bias[:, a : a + 1])
            if piece == EARLY - 1:
                nc.sync.dma_start(rows[:, :early_cols], early[:])
        nc.sync.dma_start(rows[:, early_cols:], late[:])
